import numpy as np
import ml_dtypes


def mxq(x, axis, fmt="e4m3"):
    dtype, down = {"e4m3": (ml_dtypes.float8_e4m3fn, 7), "e5m2": (ml_dtypes.float8_e5m2, 14)}[fmt]
    v = np.moveaxis(np.asarray(x, np.float32).astype(ml_dtypes.bfloat16).astype(np.float64), axis, -1)
    blocks = v.reshape(v.shape[:-1] + (-1, 32))
    amax = np.abs(blocks).max(-1, keepdims=True)
    byte = np.maximum(np.where(amax > 0, np.frexp(amax)[1] - 1 + 127, 0) - down, 1)
    scale = np.exp2(byte - 127.0)
    codes = (blocks / scale).astype(np.float32).astype(dtype).astype(np.float64)
    return np.moveaxis((codes * scale).reshape(v.shape), -1, axis)


WIDE = False


def mx_kscale(k):
    if not WIDE:
        return np.ones(k)
    levels = np.array([10, -10, 5, -5, 0])
    if k % 512:
        return np.exp2(np.random.permutation(np.resize(levels, k // 32))).repeat(32)
    a = np.empty((k // 512, 16))
    for p in range(k // 512):
        a[p, :8] = np.random.permutation(np.resize(levels, 8))
        for g in range(8):
            far = levels[np.abs(levels - a[p, g]) >= 10]
            a[p, g + 8] = far[np.random.randint(len(far))]
    return np.exp2(a.ravel()).repeat(32)


def f64(x):
    return np.asarray(x).astype(np.float64)


def striped(idx):
    return np.tile(idx.reshape(-1, 16).T, (8, 1)).astype(np.uint16)


def unstriped(offs):
    return offs[:16].T.reshape(-1).astype(np.int64)


def striped8(idx):
    return np.concatenate([x.reshape(-1, 16).T for x in idx]).astype(np.uint16)


def runs(offs, k):
    lists = np.stack([offs[16 * r : 16 * r + 16].T.reshape(-1) for r in range(8)]).astype(np.int64)
    return lists[np.arange(k) % 512 // 64]


def pack_weight(w):
    k, n = w.shape
    w = f64(np.asarray(w, np.float32).astype(ml_dtypes.bfloat16)).reshape(k // 32, 32, n)
    amax = np.abs(w).max(1)
    byte = np.clip(np.where(amax > 0, np.frexp(amax)[1] - 1 + 127 - 7, 1), 1, 254)
    scaled = (w * np.exp2(127.0 - byte)[:, None, :]).reshape(k, n).astype(np.float32)
    words = np.ascontiguousarray(scaled.reshape(k // 512, 128, 4, n).transpose(0, 1, 3, 2)).astype(ml_dtypes.float8_e4m3fn).view(np.uint8)
    return words, np.ascontiguousarray(byte.astype(np.uint8).reshape(k // 512, 16, n))


def unpack_weight(words, scales):
    g, p, n, _ = words.shape
    vals = np.ascontiguousarray(words).view(ml_dtypes.float8_e4m3fn).astype(np.float64) * np.repeat(np.exp2(scales.astype(np.float64) - 127.0), 8, axis=1)[..., None]
    return vals.transpose(0, 1, 3, 2).reshape(g * 512, n)


def relu(v):
    return np.maximum(v, 0.0)


K, T, S, N, H, U = 512, 2048, 512, 512, 512, 512


def setup_inputs():
    n = np.random.standard_normal
    s = mx_kscale(K)[:, None]
    u = mx_kscale(H)
    packed_xT = pack_weight(n((K, T)) * s)
    return {
        "x_words": packed_xT[0],
        "x_scales": packed_xT[1],
        "w1": (n((K, H)) / np.sqrt(K) / s).astype(np.float32),
        "tab": np.random.uniform(0.1, 0.8, (H, U)).astype(np.float32),
        "gn": (np.random.uniform(0.5, 1.5, (H, 1)) * u[:, None]).astype(np.float32),
        "w2": (n((H, N)) / np.sqrt(H) / u[:, None]).astype(np.float32),
        "res": (2 * n((N, S))).astype(np.float32),
        "offs": striped(np.random.permutation(T)[:S]),
        "kind": striped8(np.random.randint(0, U, (8, S))),
        "nb": striped8(np.stack([np.random.permutation(S) for _ in range(8)])),
    }


def reference(x_words, x_scales, w1, tab, gn, w2, res, offs, kind, nb):
    xq = unpack_weight(x_words, x_scales)[:, unstriped(offs)]
    y = mxq(f64(w1), 0, "e4m3").T @ xq
    d = y - (y[np.arange(H)[:, None], runs(nb, H)])
    th = f64(tab)[np.arange(H)[:, None], runs(kind, H)]
    z = f64(gn) * (relu(d - th) - relu(-1.0 * d - th))
    return f64(res) + (mxq(f64(w2), 0, "e4m3").T @ mxq(z, 0, "e4m3"))

@@ -1,0 +1,243 @@
+from contextlib import ExitStack
+
+import concourse.mybir as mybir
+
+K, T, S, N, H, U = 512, 2048, 512, 512, 512, 512
+FLOPS = 2 * K * H * S + 2 * H * N * S
+
+F32 = mybir.dt.float32
+BF16 = mybir.dt.bfloat16
+I32 = mybir.dt.int32
+U32 = mybir.dt.uint32
+U16 = mybir.dt.uint16
+U8 = mybir.dt.uint8
+FP8X4 = mybir.dt.float8_e4m3fn_x4
+ALU = mybir.AluOpType
+ACT = mybir.ActivationFunctionType
+
+P = 128
+PACK = 4
+HALF = S // 2
+LIST_HALF = HALF // 16
+
+
+def tile_picked_softthr_none_p_kernel(
+    tc, x_words, x_scales, w1, tab, gn, w2, res, offs, kind, nb, out
+):
+    nc = tc.nc
+    with ExitStack() as ctx:
+        keep = ctx.enter_context(tc.tile_pool(name="keep", bufs=1))
+        psum = ctx.enter_context(tc.psum_pool(name="psum", bufs=1))
+
+        def sb(name, shape, dtype):
+            return keep.tile(shape, dtype, name=name, align_bytes=64)
+
+        def half(h):
+            return slice(h * HALF, (h + 1) * HALF)
+
+        def list_half(h):
+            return slice(h * LIST_HALF, (h + 1) * LIST_HALF)
+
+        offs_sb = sb("offs_sb", [P, S // 16], U16)
+        nb_sb = sb("nb_sb", [P, S // 16], U16)
+        kind_sb = sb("kind_sb", [P, S // 16], U16)
+        x_all = sb("x_all", [P, T], U32)
+        xs_all = sb("xs_all", [P, T], U8)
+        gain = sb("gain", [P, PACK], F32)
+        w1_raw = [sb(f"w1_raw{h}", [P, PACK, HALF], F32) for h in range(2)]
+        w2_raw = [sb(f"w2_raw{h}", [P, PACK, HALF], F32) for h in range(2)]
+        tab_sb = [sb(f"tab{t}", [P, U], F32) for t in range(PACK)]
+        res_sb = [sb(f"res{b}", [P, 2, S], F32) for b in range(2)]
+
+        w1_rows = w1.rearrange("(p j) c -> p j c", j=PACK)
+        w2_rows = w2.rearrange("(p j) c -> p j c", j=PACK)
+        tab_rows = tab.rearrange("(p t) c -> p t c", t=PACK)
+        res_rows = res.rearrange("(c p) j -> p c j", p=P)
+        out_rows = out.rearrange("(c p) j -> p c j", p=P)
+
+        nc.vector.memset(xs_all[:].bitcast(I32), 0)
+        nc.gpsimd.dma_start(gain[:], gn.rearrange("(p t) o -> p (t o)", t=PACK))
+        nc.sync.dma_start(x_all[:].bitcast(I32), x_words[0].rearrange("p n r -> p (n r)").bitcast(I32))
+        nc.sync.dma_start(offs_sb[:], offs)
+        for q in range(4):
+            nc.scalar.dma_start(
+                xs_all[32 * q : 32 * q + 4, :].bitcast(I32), x_scales[0, 4 * q : 4 * q + 4, :].bitcast(I32)
+            )
+        for h in range(2):
+            nc.sync.dma_start(w1_raw[h][:], w1_rows[:, :, half(h)])
+        nc.sync.dma_start(nb_sb[:], nb)
+        nc.sync.dma_start(kind_sb[:], kind)
+        for t in range(3):
+            nc.sync.dma_start(tab_sb[t][:], tab_rows[:, t, :])
+        nc.sync.dma_start(w2_raw[0][:], w2_rows[:, :, half(0)])
+        nc.sync.dma_start(tab_sb[3][:], tab_rows[:, 3, :])
+        nc.sync.dma_start(w2_raw[1][:], w2_rows[:, :, half(1)])
+        for b in range(2):
+            nc.sync.dma_start(res_sb[b][:], res_rows[:, 2 * b : 2 * b + 2, :])
+
+        two_or_zero = sb("two_or_zero", [P, PACK], F32)
+        sign = sb("sign", [P, PACK], F32)
+        minus_sign = sb("minus_sign", [P, PACK], F32)
+        minus_abs = sb("minus_abs", [P, PACK], F32)
+        nc.gpsimd.tensor_scalar(two_or_zero[:], gain[:], 0.0, 2.0, ALU.is_ge, ALU.mult)
+        nc.gpsimd.tensor_scalar(sign[:], two_or_zero[:], 1.0, -1.0, ALU.mult, ALU.add)
+        nc.gpsimd.tensor_scalar(minus_sign[:], two_or_zero[:], -1.0, 1.0, ALU.mult, ALU.add)
+        nc.gpsimd.tensor_tensor(minus_abs[:], gain[:], minus_sign[:], ALU.mult)
+
+        x_pick = sb("x_pick", [P, S], U32)
+        xs_pick = sb("xs_pick", [P, S], U8)
+        nc.vector.tensor_copy(xs_pick[:], xs_all[:].indirect(offs_sb[:]))
+        nc.vector.tensor_copy(x_pick[:], x_all[:].indirect(offs_sb[:]))
+
+        w1_first = sb("w1_first", [P, P, PACK], BF16)
+        w1_rest = sb("w1_rest", [P, PACK - 1, P, PACK], BF16)
+        m_half = P // 2
+        by_tile = [w1_raw[h][:].rearrange("p j (m t) -> p m t j", t=PACK) for h in range(2)]
+
+        def weave_w1_first(h, copy):
+            copy(w1_first[:, h * m_half : (h + 1) * m_half, :], by_tile[h][:, :, 0, :])
+
+        def weave_w1_rest(h, copy):
+            copy(
+                w1_rest[:, :, h * m_half : (h + 1) * m_half, :].rearrange("p t m j -> p m t j"),
+                by_tile[h][:, :, 1:PACK, :],
+            )
+
+        w1_codes = [sb(f"w1_codes{t}", [P, P], U32) for t in range(PACK)]
+        w1_scales = [sb(f"w1_scales{t}", [P, P], U8) for t in range(PACK)]
+
+        def quantize_w1(t):
+            source = w1_first[:] if t == 0 else w1_rest[:, t - 1]
+            nc.vector.quantize_mx(
+                out=w1_codes[t][:].bitcast(FP8X4), scales=w1_scales[t][:], in_=source.rearrange("p m j -> p (m j)")
+            )
+
+        def project(bank, t, cols):
+            nc.tensor.matmul_mx(
+                out=bank[:], lhsT=w1_codes[t][:].bitcast(FP8X4), lhsT_scale=w1_scales[t][:],
+                rhs=x_pick[:, cols].bitcast(FP8X4), rhs_scale=xs_pick[:, cols], start=True, stop=True,
+            )
+
+        y_win = [sb(f"y_win{t}", [P, S], F32) for t in range(PACK)]
+        y_dup = [[sb(f"y_dup{t}_{h}", [P, HALF], F32) for h in range(2)] for t in range(1)]
+        y_full = [sb(f"y_full{t}", [P, S], F32) for t in range(1, PACK)]
+
+        weave_w1_first(0, nc.scalar.copy)
+        weave_w1_rest(0, nc.scalar.copy)
+        weave_w1_first(1, nc.vector.tensor_copy)
+        weave_w1_rest(1, nc.scalar.copy)
+        quantize_w1(0)
+        first_banks = [psum.tile([P, HALF], F32, name=f"y0_ps{h}", tag=f"bank{h}") for h in range(2)]
+        for h in range(2):
+            project(first_banks[h], 0, half(h))
+        y_ps = [None]
+        for t in range(1, PACK):
+            quantize_w1(t)
+            bank = psum.tile([P, S], F32, name=f"y_ps{t}", tag=f"bank{t + 1}")
+            project(bank, t, slice(0, S))
+            y_ps.append(bank)
+        for h in range(2):
+            nc.scalar.activation(y_win[0][:, half(h)], first_banks[h][:], ACT.Copy, scale=sign[:, 0:1])
+        nc.vector.tensor_scalar(y_dup[0][0][:], first_banks[0][:], sign[:, 0:1], None, ALU.mult)
+        nc.scalar.activation(y_dup[0][1][:], first_banks[1][:], ACT.Copy, scale=sign[:, 0:1])
+
+        def leave_psum(t):
+            nc.scalar.activation(y_win[t][:], y_ps[t][:], ACT.Copy, scale=sign[:, t : t + 1])
+            nc.scalar.copy(y_full[t - 1][:], y_win[t][:])
+
+        shrunk = [sb(f"shrunk{h}", [P, PACK, 2, HALF], F32) for h in range(2)]
+        w2_bf = [sb(f"w2_bf{h}", [P, HALF, PACK], BF16) for h in range(2)]
+        w2_codes = [sb(f"w2_codes{h}", [P, HALF], U32) for h in range(2)]
+        w2_scales = [sb(f"w2_scales{h}", [P, HALF], U8) for h in range(2)]
+
+        def weave_w2(h):
+            nc.scalar.copy(
+                w2_bf[h][:].rearrange("p (c i) j -> p c j i", i=4),
+                w2_raw[h][:].rearrange("p j (c i) -> p c j i", i=4),
+            )
+
+        def quantize_w2(h):
+            nc.vector.quantize_mx(
+                out=w2_codes[h][:].bitcast(FP8X4), scales=w2_scales[h][:],
+                in_=w2_bf[h][:].rearrange("p m j -> p (m j)"),
+            )
+
+        gaps = [[sb(f"gaps{t}_{h}", [P, 2, HALF], F32) for h in range(2)] for t in range(PACK)]
+
+        def look_up(t):
+            minus_d = [sb(f"minus_d{t}_{h}", [P, HALF], F32) for h in range(2)]
+            for h in range(2):
+                own = y_dup[0][h][:] if t == 0 else y_full[t - 1][:, half(h)]
+                nc.vector.tensor_tensor(minus_d[h][:], y_win[t][:].indirect(nb_sb[:, list_half(h)]), own, ALU.subtract)
+            for h in range(2):
+                nc.vector.tensor_tensor(
+                    gaps[t][h][:, 0, :], tab_sb[t][:].indirect(kind_sb[:, list_half(h)]), minus_d[h][:], ALU.add
+                )
+            for h in range(2):
+                nc.vector.scalar_tensor_tensor(
+                    gaps[t][h][:, 1, :], minus_d[h][:], -2.0, gaps[t][h][:, 0, :], ALU.mult, ALU.add
+                )
+            return minus_d
+
+        def shrink(t):
+            for h in range(2):
+                nc.scalar.activation(shrunk[h][:, t], gaps[t][h][:], ACT.Relu, scale=minus_abs[:, t : t + 1])
+
+        leave_psum(1)
+        md0 = look_up(0)
+
+        leave_psum(2)
+        look_up(1)
+        shrink(0)
+        leave_psum(3)
+        look_up(2)
+        shrink(1)
+        weave_w2(0)
+        look_up(3)
+        shrink(2)
+        weave_w2(1)
+        shrink(3)
+
+        z_bf = [sb(f"z_bf{h}", [P, HALF, PACK], BF16) for h in range(2)]
+        z_codes = [sb(f"z_codes{h}", [P, HALF], U32) for h in range(2)]
+        z_scales = [sb(f"z_scales{h}", [P, HALF], U8) for h in range(2)]
+        o_tags = ["bank5", "bank6", "bank7", "bank0"]
+        o_ps = {}
+
+        def make_z(h):
+            nc.vector.tensor_tensor(
+                z_bf[h][:].rearrange("p (c i) t -> p c t i", i=4),
+                shrunk[h][:, :, 0, :].rearrange("p t (c i) -> p c t i", i=4),
+                shrunk[h][:, :, 1, :].rearrange("p t (c i) -> p c t i", i=4),
+                ALU.subtract,
+            )
+
+        def second_product(h):
+            nc.vector.quantize_mx(
+                out=z_codes[h][:].bitcast(FP8X4), scales=z_scales[h][:], in_=z_bf[h][:].rearrange("p j t -> p (j t)")
+            )
+            for b in range(2):
+                bank = psum.tile([P, 2, HALF], F32, name=f"o_ps{h}_{b}", tag=o_tags[2 * h + b])
+                for c in range(2):
+                    cols = slice(c * P, (c + 1) * P)
+                    nc.tensor.matmul_mx(
+                        out=bank[:, c, :], lhsT=w2_codes[b][:, cols].bitcast(FP8X4), lhsT_scale=w2_scales[b][:, cols],
+                        rhs=z_codes[h][:].bitcast(FP8X4), rhs_scale=z_scales[h][:], start=True, stop=True,
+                    )
+                o_ps[h, b] = bank
+
+        def leave(h, b, queue):
+            o_sb = sb(f"o_sb{h}_{b}", [P, 2, HALF], F32)
+            nc.vector.tensor_tensor(o_sb[:], o_ps[h, b][:], res_sb[b][:, :, half(h)], ALU.add)
+            queue.dma_start(out_rows[:, 2 * b : 2 * b + 2, half(h)], o_sb[:])
+
+        quantize_w2(0)
+        make_z(0)
+        quantize_w2(1)
+        second_product(0)
+        make_z(1)
+        leave(0, 0, nc.sync)
+        second_product(1)
+        leave(0, 1, nc.sync)
+        leave(1, 0, nc.sync)
+        leave(1, 1, nc.scalar)

@@ -29,8 +29,8 @@ def tile_picked_softthr_none_p_kernel(
         keep = ctx.enter_context(tc.tile_pool(name="keep", bufs=1))
         psum = ctx.enter_context(tc.psum_pool(name="psum", bufs=1))
 
-        def sb(name, shape, dtype):
-            return keep.tile(shape, dtype, name=name, align_bytes=64)
+        def sb(name, shape, dtype, tag=None):
+            return keep.tile(shape, dtype, name=name, tag=tag or name, align_bytes=64)
 
         def half(h):
             return slice(h * HALF, (h + 1) * HALF)
@@ -44,30 +44,29 @@ def tile_picked_softthr_none_p_kernel(
         x_all = sb("x_all", [P, T], U32)
         xs_all = sb("xs_all", [P, T], U8)
         gain = sb("gain", [P, PACK], F32)
-        w1_raw = [sb(f"w1_raw{h}", [P, PACK, HALF], F32) for h in range(2)]
+        w1_raw = sb("w1_raw", [P, PACK, H], F32)
         w2_raw = [sb(f"w2_raw{h}", [P, PACK, HALF], F32) for h in range(2)]
         tab_sb = [sb(f"tab{t}", [P, U], F32) for t in range(PACK)]
         res_sb = [sb(f"res{b}", [P, 2, S], F32) for b in range(2)]
 
-        w1_rows = w1.rearrange("(p j) c -> p j c", j=PACK)
         w2_rows = w2.rearrange("(p j) c -> p j c", j=PACK)
         tab_rows = tab.rearrange("(p t) c -> p t c", t=PACK)
         res_rows = res.rearrange("(c p) j -> p c j", p=P)
         out_rows = out.rearrange("(c p) j -> p c j", p=P)
 
         nc.vector.memset(xs_all[:].bitcast(I32), 0)
-        nc.gpsimd.dma_start(gain[:], gn.rearrange("(p t) o -> p (t o)", t=PACK))
-        nc.sync.dma_start(x_all[:].bitcast(I32), x_words[0].rearrange("p n r -> p (n r)").bitcast(I32))
+        nc.scalar.dma_start(gain[:], gn.rearrange("(p t) o -> p (t o)", t=PACK))
         nc.sync.dma_start(offs_sb[:], offs)
+        nc.sync.dma_start(kind_sb[:], kind)
+        nc.sync.dma_start(nb_sb[:], nb)
         for q in range(4):
             nc.scalar.dma_start(
                 xs_all[32 * q : 32 * q + 4, :].bitcast(I32), x_scales[0, 4 * q : 4 * q + 4, :].bitcast(I32)
             )
-        for h in range(2):
-            nc.sync.dma_start(w1_raw[h][:], w1_rows[:, :, half(h)])
-        nc.sync.dma_start(nb_sb[:], nb)
-        nc.sync.dma_start(kind_sb[:], kind)
-        for t in range(3):
+        nc.sync.dma_start(w1_raw[:], w1.rearrange("(p j) c -> p j c", j=PACK))
+        nc.sync.dma_start(x_all[:].bitcast(I32), x_words[0].rearrange("p n r -> p (n r)").bitcast(I32))
+        nc.sync.dma_start(tab_sb[0][:], tab_rows[:, 0, :])
+        for t in range(1, 3):
             nc.sync.dma_start(tab_sb[t][:], tab_rows[:, t, :])
         nc.sync.dma_start(w2_raw[0][:], w2_rows[:, :, half(0)])
         nc.sync.dma_start(tab_sb[3][:], tab_rows[:, 3, :])
@@ -75,75 +74,61 @@ def tile_picked_softthr_none_p_kernel(
         for b in range(2):
             nc.sync.dma_start(res_sb[b][:], res_rows[:, 2 * b : 2 * b + 2, :])
 
+        xs_pick = sb("xs_pick", [P, S], U8)
+
         two_or_zero = sb("two_or_zero", [P, PACK], F32)
         sign = sb("sign", [P, PACK], F32)
-        minus_sign = sb("minus_sign", [P, PACK], F32)
         minus_abs = sb("minus_abs", [P, PACK], F32)
+        minus_sign = sb("minus_sign", [P, PACK], F32)
         nc.gpsimd.tensor_scalar(two_or_zero[:], gain[:], 0.0, 2.0, ALU.is_ge, ALU.mult)
         nc.gpsimd.tensor_scalar(sign[:], two_or_zero[:], 1.0, -1.0, ALU.mult, ALU.add)
         nc.gpsimd.tensor_scalar(minus_sign[:], two_or_zero[:], -1.0, 1.0, ALU.mult, ALU.add)
         nc.gpsimd.tensor_tensor(minus_abs[:], gain[:], minus_sign[:], ALU.mult)
 
-        x_pick = sb("x_pick", [P, S], U32)
-        xs_pick = sb("xs_pick", [P, S], U8)
+        w1_bf = sb("w1_bf", [P, PACK, P, PACK], BF16)
+        m_half = 80
+        w1_by_tile = w1_raw[:].rearrange("p j (m t) -> p m t j", t=PACK)
+        w1_woven = w1_bf[:].rearrange("p t m j -> p m t j")
+        nc.scalar.copy(w1_woven[:, 0:m_half], w1_by_tile[:, 0:m_half])
+        nc.vector.tensor_copy(w1_woven[:, m_half:P], w1_by_tile[:, m_half:P])
         nc.vector.tensor_copy(xs_pick[:], xs_all[:].indirect(offs_sb[:]))
-        nc.vector.tensor_copy(x_pick[:], x_all[:].indirect(offs_sb[:]))
+        w1_codes = sb("w1_codes", [P, H], U32)
+        w1_scales = sb("w1_scales", [P, H], U8)
+        nc.vector.quantize_mx(
+            out=w1_codes[:].bitcast(FP8X4), scales=w1_scales[:], in_=w1_bf[:].rearrange("p t m j -> p (t m j)")
+        )
+        x_pick = sb("x_pick", [P, S], U32, tag="w1_bf")
+        for h in range(2):
+            nc.vector.tensor_copy(x_pick[:, half(h)], x_all[:].indirect(offs_sb[:, list_half(h)]))
 
-        w1_first = sb("w1_first", [P, P, PACK], BF16)
-        w1_rest = sb("w1_rest", [P, PACK - 1, P, PACK], BF16)
-        m_half = P // 2
-        by_tile = [w1_raw[h][:].rearrange("p j (m t) -> p m t j", t=PACK) for h in range(2)]
-
-        def weave_w1_first(h, copy):
-            copy(w1_first[:, h * m_half : (h + 1) * m_half, :], by_tile[h][:, :, 0, :])
-
-        def weave_w1_rest(h, copy):
-            copy(
-                w1_rest[:, :, h * m_half : (h + 1) * m_half, :].rearrange("p t m j -> p m t j"),
-                by_tile[h][:, :, 1:PACK, :],
-            )
-
-        w1_codes = [sb(f"w1_codes{t}", [P, P], U32) for t in range(PACK)]
-        w1_scales = [sb(f"w1_scales{t}", [P, P], U8) for t in range(PACK)]
-
-        def quantize_w1(t):
-            source = w1_first[:] if t == 0 else w1_rest[:, t - 1]
-            nc.vector.quantize_mx(
-                out=w1_codes[t][:].bitcast(FP8X4), scales=w1_scales[t][:], in_=source.rearrange("p m j -> p (m j)")
-            )
-
-        def project(bank, t, cols):
+        def project(target, t, places):
+            cols = slice(t * P, (t + 1) * P)
             nc.tensor.matmul_mx(
-                out=bank[:], lhsT=w1_codes[t][:].bitcast(FP8X4), lhsT_scale=w1_scales[t][:],
-                rhs=x_pick[:, cols].bitcast(FP8X4), rhs_scale=xs_pick[:, cols], start=True, stop=True,
+                out=target, lhsT=w1_codes[:, cols].bitcast(FP8X4), lhsT_scale=w1_scales[:, cols],
+                rhs=x_pick[:, places].bitcast(FP8X4), rhs_scale=xs_pick[:, places], start=True, stop=True,
             )
 
         y_win = [sb(f"y_win{t}", [P, S], F32) for t in range(PACK)]
         y_dup = [[sb(f"y_dup{t}_{h}", [P, HALF], F32) for h in range(2)] for t in range(1)]
         y_full = [sb(f"y_full{t}", [P, S], F32) for t in range(1, PACK)]
 
-        weave_w1_first(0, nc.scalar.copy)
-        weave_w1_rest(0, nc.scalar.copy)
-        weave_w1_first(1, nc.vector.tensor_copy)
-        weave_w1_rest(1, nc.scalar.copy)
-        quantize_w1(0)
         first_banks = [psum.tile([P, HALF], F32, name=f"y0_ps{h}", tag=f"bank{h}") for h in range(2)]
         for h in range(2):
-            project(first_banks[h], 0, half(h))
+            project(first_banks[h][:], 0, half(h))
         y_ps = [None]
         for t in range(1, PACK):
-            quantize_w1(t)
             bank = psum.tile([P, S], F32, name=f"y_ps{t}", tag=f"bank{t + 1}")
-            project(bank, t, slice(0, S))
+            project(bank[:], t, slice(0, S))
             y_ps.append(bank)
+        first_th = sb("first_th", [P, S], F32, tag="x_all")
         for h in range(2):
             nc.scalar.activation(y_win[0][:, half(h)], first_banks[h][:], ACT.Copy, scale=sign[:, 0:1])
-        nc.vector.tensor_scalar(y_dup[0][0][:], first_banks[0][:], sign[:, 0:1], None, ALU.mult)
-        nc.scalar.activation(y_dup[0][1][:], first_banks[1][:], ACT.Copy, scale=sign[:, 0:1])
+            nc.scalar.activation(y_dup[0][h][:], first_banks[h][:], ACT.Copy, scale=sign[:, 0:1])
+            nc.vector.tensor_copy(first_th[:, half(h)], tab_sb[0][:].indirect(kind_sb[:, list_half(h)]))
 
         def leave_psum(t):
             nc.scalar.activation(y_win[t][:], y_ps[t][:], ACT.Copy, scale=sign[:, t : t + 1])
-            nc.scalar.copy(y_full[t - 1][:], y_win[t][:])
+            nc.scalar.activation(y_full[t - 1][:], y_ps[t][:], ACT.Copy, scale=sign[:, t : t + 1])
 
         shrunk = [sb(f"shrunk{h}", [P, PACK, 2, HALF], F32) for h in range(2)]
         w2_bf = [sb(f"w2_bf{h}", [P, HALF, PACK], BF16) for h in range(2)]
@@ -169,6 +154,11 @@ def tile_picked_softthr_none_p_kernel(
             for h in range(2):
                 own = y_dup[0][h][:] if t == 0 else y_full[t - 1][:, half(h)]
                 nc.vector.tensor_tensor(minus_d[h][:], y_win[t][:].indirect(nb_sb[:, list_half(h)]), own, ALU.subtract)
+            if t == 0:
+                for h in range(2):
+                    nc.vector.tensor_tensor(gaps[t][h][:, 0, :], first_th[:, half(h)], minus_d[h][:], ALU.add)
+                    nc.vector.tensor_tensor(gaps[t][h][:, 1, :], first_th[:, half(h)], minus_d[h][:], ALU.subtract)
+                return minus_d
             for h in range(2):
                 nc.vector.tensor_tensor(
                     gaps[t][h][:, 0, :], tab_sb[t][:].indirect(kind_sb[:, list_half(h)]), minus_d[h][:], ALU.add
@@ -201,7 +191,7 @@ def tile_picked_softthr_none_p_kernel(
         z_bf = [sb(f"z_bf{h}", [P, HALF, PACK], BF16) for h in range(2)]
         z_codes = [sb(f"z_codes{h}", [P, HALF], U32) for h in range(2)]
         z_scales = [sb(f"z_scales{h}", [P, HALF], U8) for h in range(2)]
-        o_tags = ["bank5", "bank6", "bank7", "bank0"]
+        o_tags = {0: ["bank5", "bank6"], 1: ["bank7", "bank0", "bank1", "bank2"]}
         o_ps = {}
 
         def make_z(h):
@@ -216,20 +206,27 @@ def tile_picked_softthr_none_p_kernel(
             nc.vector.quantize_mx(
                 out=z_codes[h][:].bitcast(FP8X4), scales=z_scales[h][:], in_=z_bf[h][:].rearrange("p j t -> p (j t)")
             )
-            for b in range(2):
-                bank = psum.tile([P, 2, HALF], F32, name=f"o_ps{h}_{b}", tag=o_tags[2 * h + b])
-                for c in range(2):
-                    cols = slice(c * P, (c + 1) * P)
+            tiles = PACK // len(o_tags[h])
+            for b, tag in enumerate(o_tags[h]):
+                bank = psum.tile([P, tiles, HALF], F32, name=f"o_ps{h}_{b}", tag=tag)
+                for c in range(tiles):
+                    w_half, first = divmod((b * tiles + c) * P, HALF)
+                    cols = slice(first, first + P)
                     nc.tensor.matmul_mx(
-                        out=bank[:, c, :], lhsT=w2_codes[b][:, cols].bitcast(FP8X4), lhsT_scale=w2_scales[b][:, cols],
+                        out=bank[:, c, :], lhsT=w2_codes[w_half][:, cols].bitcast(FP8X4),
+                        lhsT_scale=w2_scales[w_half][:, cols],
                         rhs=z_codes[h][:].bitcast(FP8X4), rhs_scale=z_scales[h][:], start=True, stop=True,
                     )
                 o_ps[h, b] = bank
 
         def leave(h, b, queue):
-            o_sb = sb(f"o_sb{h}_{b}", [P, 2, HALF], F32)
-            nc.vector.tensor_tensor(o_sb[:], o_ps[h, b][:], res_sb[b][:, :, half(h)], ALU.add)
-            queue.dma_start(out_rows[:, 2 * b : 2 * b + 2, half(h)], o_sb[:])
+            tiles = PACK // len(o_tags[h])
+            pair, first = divmod(b * tiles, 2)
+            o_sb = sb(f"o_sb{h}_{b}", [P, tiles, HALF], F32)
+            nc.vector.tensor_tensor(
+                o_sb[:], o_ps[h, b][:], res_sb[pair][:, first : first + tiles, half(h)], ALU.add
+            )
+            queue.dma_start(out_rows[:, b * tiles : (b + 1) * tiles, half(h)], o_sb[:])
 
         quantize_w2(0)
         make_z(0)
@@ -239,5 +236,5 @@ def tile_picked_softthr_none_p_kernel(
         leave(0, 0, nc.sync)
         second_product(1)
         leave(0, 1, nc.sync)
-        leave(1, 0, nc.sync)
-        leave(1, 1, nc.scalar)
+        for b in range(PACK):
+            leave(1, b, nc.scalar if b % 2 else nc.sync)

@@ -54,18 +54,19 @@ def tile_picked_softthr_none_p_kernel(
         res_rows = res.rearrange("(c p) j -> p c j", p=P)
         out_rows = out.rearrange("(c p) j -> p c j", p=P)
 
-        nc.vector.memset(xs_all[:].bitcast(I32), 0)
+        nc.vector.memset(xs_all[:, 0 : T // 2].bitcast(I32), 0)
+        nc.gpsimd.memset(xs_all[:, T // 2 : T].bitcast(I32), 0)
         nc.scalar.dma_start(gain[:], gn.rearrange("(p t) o -> p (t o)", t=PACK))
-        nc.sync.dma_start(offs_sb[:], offs)
-        nc.sync.dma_start(kind_sb[:], kind)
-        nc.sync.dma_start(nb_sb[:], nb)
+        nc.sync.dma_start(w1_raw[:], w1.rearrange("(p j) c -> p j c", j=PACK))
         for q in range(4):
-            nc.scalar.dma_start(
+            nc.sync.dma_start(
                 xs_all[32 * q : 32 * q + 4, :].bitcast(I32), x_scales[0, 4 * q : 4 * q + 4, :].bitcast(I32)
             )
-        nc.sync.dma_start(w1_raw[:], w1.rearrange("(p j) c -> p j c", j=PACK))
+        nc.sync.dma_start(offs_sb[:], offs)
         nc.sync.dma_start(x_all[:].bitcast(I32), x_words[0].rearrange("p n r -> p (n r)").bitcast(I32))
+        nc.sync.dma_start(kind_sb[:], kind)
         nc.sync.dma_start(tab_sb[0][:], tab_rows[:, 0, :])
+        nc.sync.dma_start(nb_sb[:], nb)
         for t in range(1, 3):
             nc.sync.dma_start(tab_sb[t][:], tab_rows[:, t, :])
         nc.sync.dma_start(w2_raw[0][:], w2_rows[:, :, half(0)])
@@ -92,7 +93,7 @@ def tile_picked_softthr_none_p_kernel(
         nc.scalar.copy(w1_woven[:, 0:m_half], w1_by_tile[:, 0:m_half])
         nc.vector.tensor_copy(w1_woven[:, m_half:P], w1_by_tile[:, m_half:P])
         nc.vector.tensor_copy(xs_pick[:], xs_all[:].indirect(offs_sb[:]))
-        w1_codes = sb("w1_codes", [P, H], U32)
+        w1_codes = sb("w1_codes", [P, H], U32, tag="xs_all")
         w1_scales = sb("w1_scales", [P, H], U8)
         nc.vector.quantize_mx(
             out=w1_codes[:].bitcast(FP8X4), scales=w1_scales[:], in_=w1_bf[:].rearrange("p t m j -> p (t m j)")
@@ -185,8 +186,8 @@ def tile_picked_softthr_none_p_kernel(
         weave_w2(0)
         look_up(3)
         shrink(2)
-        weave_w2(1)
         shrink(3)
+        weave_w2(1)
 
         z_bf = [sb(f"z_bf{h}", [P, HALF, PACK], BF16) for h in range(2)]
         z_codes = [sb(f"z_codes{h}", [P, HALF], U32) for h in range(2)]
@@ -202,22 +203,23 @@ def tile_picked_softthr_none_p_kernel(
                 ALU.subtract,
             )
 
-        def second_product(h):
+        def quantize_z(h):
             nc.vector.quantize_mx(
                 out=z_codes[h][:].bitcast(FP8X4), scales=z_scales[h][:], in_=z_bf[h][:].rearrange("p j t -> p (j t)")
             )
+
+        def second_product(h, b):
             tiles = PACK // len(o_tags[h])
-            for b, tag in enumerate(o_tags[h]):
-                bank = psum.tile([P, tiles, HALF], F32, name=f"o_ps{h}_{b}", tag=tag)
-                for c in range(tiles):
-                    w_half, first = divmod((b * tiles + c) * P, HALF)
-                    cols = slice(first, first + P)
-                    nc.tensor.matmul_mx(
-                        out=bank[:, c, :], lhsT=w2_codes[w_half][:, cols].bitcast(FP8X4),
-                        lhsT_scale=w2_scales[w_half][:, cols],
-                        rhs=z_codes[h][:].bitcast(FP8X4), rhs_scale=z_scales[h][:], start=True, stop=True,
-                    )
-                o_ps[h, b] = bank
+            bank = psum.tile([P, tiles, HALF], F32, name=f"o_ps{h}_{b}", tag=o_tags[h][b])
+            for c in range(tiles):
+                w_half, first = divmod((b * tiles + c) * P, HALF)
+                cols = slice(first, first + P)
+                nc.tensor.matmul_mx(
+                    out=bank[:, c, :], lhsT=w2_codes[w_half][:, cols].bitcast(FP8X4),
+                    lhsT_scale=w2_scales[w_half][:, cols],
+                    rhs=z_codes[h][:].bitcast(FP8X4), rhs_scale=z_scales[h][:], start=True, stop=True,
+                )
+            o_ps[h, b] = bank
 
         def leave(h, b, queue):
             tiles = PACK // len(o_tags[h])
@@ -230,11 +232,15 @@ def tile_picked_softthr_none_p_kernel(
 
         quantize_w2(0)
         make_z(0)
-        quantize_w2(1)
-        second_product(0)
+        quantize_z(0)
+        second_product(0, 0)
         make_z(1)
+        quantize_w2(1)
+        second_product(0, 1)
         leave(0, 0, nc.sync)
-        second_product(1)
+        quantize_z(1)
+        for b in range(PACK):
+            second_product(1, b)
         leave(0, 1, nc.sync)
         for b in range(PACK):
             leave(1, b, nc.scalar if b % 2 else nc.sync)

@@ -1,6 +1,7 @@
 from contextlib import ExitStack
 
 import concourse.mybir as mybir
+from concourse.masks import make_identity
 
 K, T, S, N, H, U = 512, 2048, 512, 512, 512, 512
 FLOPS = 2 * K * H * S + 2 * H * N * S
@@ -19,6 +20,8 @@ P = 128
 PACK = 4
 HALF = S // 2
 LIST_HALF = HALF // 16
+SCALAR_SHARE = 64
+EARLY_TABLES = 3
 
 
 def tile_picked_softthr_none_p_kernel(
@@ -56,7 +59,12 @@ def tile_picked_softthr_none_p_kernel(
 
         nc.vector.memset(xs_all[:, 0 : T // 2].bitcast(I32), 0)
         nc.gpsimd.memset(xs_all[:, T // 2 : T].bitcast(I32), 0)
+        identity = sb("identity", [P, P], F32)
+        make_identity(nc, identity[:])
         nc.scalar.dma_start(gain[:], gn.rearrange("(p t) o -> p (t o)", t=PACK))
+        nc.sync.dma_start(kind_sb[:], kind)
+        for t in range(EARLY_TABLES):
+            nc.sync.dma_start(tab_sb[t][:], tab_rows[:, t, :])
         nc.sync.dma_start(w1_raw[:], w1.rearrange("(p j) c -> p j c", j=PACK))
         for q in range(4):
             nc.sync.dma_start(
@@ -64,34 +72,48 @@ def tile_picked_softthr_none_p_kernel(
             )
         nc.sync.dma_start(offs_sb[:], offs)
         nc.sync.dma_start(x_all[:].bitcast(I32), x_words[0].rearrange("p n r -> p (n r)").bitcast(I32))
-        nc.sync.dma_start(kind_sb[:], kind)
-        nc.sync.dma_start(tab_sb[0][:], tab_rows[:, 0, :])
-        nc.sync.dma_start(nb_sb[:], nb)
-        for t in range(1, 3):
+        for t in range(EARLY_TABLES, PACK):
             nc.sync.dma_start(tab_sb[t][:], tab_rows[:, t, :])
-        nc.sync.dma_start(w2_raw[0][:], w2_rows[:, :, half(0)])
-        nc.sync.dma_start(tab_sb[3][:], tab_rows[:, 3, :])
-        nc.sync.dma_start(w2_raw[1][:], w2_rows[:, :, half(1)])
+        nc.sync.dma_start(nb_sb[:], nb)
+        for h in range(2):
+            nc.sync.dma_start(w2_raw[h][:], w2_rows[:, :, half(h)])
         for b in range(2):
             nc.sync.dma_start(res_sb[b][:], res_rows[:, 2 * b : 2 * b + 2, :])
 
-        xs_pick = sb("xs_pick", [P, S], U8)
+        early = [(0, 0), (1, 0), (2, 0), (0, 1), (1, 1)]
+        late = [(3, 0), (2, 1), (3, 1)]
+        th = {(t, h): sb(f"th{t}_{h}", [P, HALF], F32)[:] for t, h in early}
 
-        two_or_zero = sb("two_or_zero", [P, PACK], F32)
-        sign = sb("sign", [P, PACK], F32)
+        def fetch_thresholds(t, h):
+            nc.vector.tensor_copy(th[t, h], tab_sb[t][:].indirect(kind_sb[:, list_half(h)]))
+
+        minus_gain = sb("minus_gain", [P, PACK], F32)
+        abs_gain = sb("abs_gain", [P, PACK], F32)
         minus_abs = sb("minus_abs", [P, PACK], F32)
-        minus_sign = sb("minus_sign", [P, PACK], F32)
-        nc.gpsimd.tensor_scalar(two_or_zero[:], gain[:], 0.0, 2.0, ALU.is_ge, ALU.mult)
-        nc.gpsimd.tensor_scalar(sign[:], two_or_zero[:], 1.0, -1.0, ALU.mult, ALU.add)
-        nc.gpsimd.tensor_scalar(minus_sign[:], two_or_zero[:], -1.0, 1.0, ALU.mult, ALU.add)
-        nc.gpsimd.tensor_tensor(minus_abs[:], gain[:], minus_sign[:], ALU.mult)
+        nc.gpsimd.tensor_scalar(minus_gain[:], gain[:], -1.0, 0.0, ALU.mult, ALU.add)
+        nc.scalar.activation(abs_gain[:], gain[:], ACT.Abs)
+        nc.gpsimd.tensor_scalar(minus_abs[:], abs_gain[:], -1.0, 0.0, ALU.mult, ALU.add)
+        signed_th = {(t, s): sb(f"signed_th{t}_{s}", [P, HALF], F32)[:] for t in (0,) for s in range(2)}
+
+        def scale_thresholds(t):
+            for s, factor in enumerate((minus_abs, abs_gain)):
+                nc.scalar.activation(signed_th[t, s], th[t, 0], ACT.Copy, scale=factor[:, t : t + 1])
+
+        for t, h in early:
+            fetch_thresholds(t, h)
+        scale_thresholds(0)
 
         w1_bf = sb("w1_bf", [P, PACK, P, PACK], BF16)
-        m_half = 80
         w1_by_tile = w1_raw[:].rearrange("p j (m t) -> p m t j", t=PACK)
         w1_woven = w1_bf[:].rearrange("p t m j -> p m t j")
-        nc.scalar.copy(w1_woven[:, 0:m_half], w1_by_tile[:, 0:m_half])
-        nc.vector.tensor_copy(w1_woven[:, m_half:P], w1_by_tile[:, m_half:P])
+        nc.scalar.copy(w1_woven[:, 0:SCALAR_SHARE], w1_by_tile[:, 0:SCALAR_SHARE])
+        nc.vector.tensor_copy(w1_woven[:, SCALAR_SHARE:P], w1_by_tile[:, SCALAR_SHARE:P])
+        signed_mid = sb("signed_mid", [P, 2, 2, HALF], F32, tag="w1_raw")
+        for t in (1, 2):
+            for s in range(2):
+                signed_th[t, s] = signed_mid[:, t - 1, s, :]
+            scale_thresholds(t)
+        xs_pick = sb("xs_pick", [P, S], U8)
         nc.vector.tensor_copy(xs_pick[:], xs_all[:].indirect(offs_sb[:]))
         w1_codes = sb("w1_codes", [P, H], U32, tag="xs_all")
         w1_scales = sb("w1_scales", [P, H], U8)
@@ -99,8 +121,11 @@ def tile_picked_softthr_none_p_kernel(
             out=w1_codes[:].bitcast(FP8X4), scales=w1_scales[:], in_=w1_bf[:].rearrange("p t m j -> p (t m j)")
         )
         x_pick = sb("x_pick", [P, S], U32, tag="w1_bf")
-        for h in range(2):
+        for h in (1, 0):
             nc.vector.tensor_copy(x_pick[:, half(h)], x_all[:].indirect(offs_sb[:, list_half(h)]))
+        th_late = sb("th_late", [P, len(late), HALF], F32, tag="x_all")
+        for place, key in enumerate(late):
+            th[key] = th_late[:, place, :]
 
         def project(target, t, places):
             cols = slice(t * P, (t + 1) * P)
@@ -110,33 +135,34 @@ def tile_picked_softthr_none_p_kernel(
             )
 
         y_win = [sb(f"y_win{t}", [P, S], F32) for t in range(PACK)]
-        y_dup = [[sb(f"y_dup{t}_{h}", [P, HALF], F32) for h in range(2)] for t in range(1)]
-        y_full = [sb(f"y_full{t}", [P, S], F32) for t in range(1, PACK)]
+        y_own = [sb(f"y_own{t}", [P, S], F32) for t in range(PACK)]
 
         first_banks = [psum.tile([P, HALF], F32, name=f"y0_ps{h}", tag=f"bank{h}") for h in range(2)]
-        for h in range(2):
+        for h in (1, 0):
             project(first_banks[h][:], 0, half(h))
         y_ps = [None]
         for t in range(1, PACK):
             bank = psum.tile([P, S], F32, name=f"y_ps{t}", tag=f"bank{t + 1}")
             project(bank[:], t, slice(0, S))
             y_ps.append(bank)
-        first_th = sb("first_th", [P, S], F32, tag="x_all")
-        for h in range(2):
-            nc.scalar.activation(y_win[0][:, half(h)], first_banks[h][:], ACT.Copy, scale=sign[:, 0:1])
-            nc.scalar.activation(y_dup[0][h][:], first_banks[h][:], ACT.Copy, scale=sign[:, 0:1])
-            nc.vector.tensor_copy(first_th[:, half(h)], tab_sb[0][:].indirect(kind_sb[:, list_half(h)]))
+        for t, h in late:
+            fetch_thresholds(t, h)
+        for h in (1, 0):
+            for copy in (y_win[0], y_own[0]):
+                nc.scalar.activation(copy[:, half(h)], first_banks[h][:], ACT.Copy, scale=minus_gain[:, 0:1])
+        for t in range(1, PACK):
+            for copy in (y_win[t], y_own[t]):
+                nc.scalar.activation(copy[:], y_ps[t][:], ACT.Copy, scale=minus_gain[:, t : t + 1])
+            if t == 1:
+                signed_late = sb("signed_late", [P, 2, HALF], F32, tag="xs_pick")
+                for s in range(2):
+                    signed_th[EARLY_TABLES, s] = signed_late[:, s, :]
+                scale_thresholds(EARLY_TABLES)
 
-        def leave_psum(t):
-            nc.scalar.activation(y_win[t][:], y_ps[t][:], ACT.Copy, scale=sign[:, t : t + 1])
-            nc.scalar.activation(y_full[t - 1][:], y_ps[t][:], ACT.Copy, scale=sign[:, t : t + 1])
-
-        shrunk = [sb(f"shrunk{h}", [P, PACK, 2, HALF], F32) for h in range(2)]
-        w2_bf = [sb(f"w2_bf{h}", [P, HALF, PACK], BF16) for h in range(2)]
+        w2_bf = [sb(f"w2_bf{h}", [P, HALF, PACK], BF16, tag=("w1_bf", "xs_all")[h]) for h in range(2)]
         w2_codes = [sb(f"w2_codes{h}", [P, HALF], U32) for h in range(2)]
         w2_scales = [sb(f"w2_scales{h}", [P, HALF], U8) for h in range(2)]
-
-        def weave_w2(h):
+        for h in range(2):
             nc.scalar.copy(
                 w2_bf[h][:].rearrange("p (c i) j -> p c j i", i=4),
                 w2_raw[h][:].rearrange("p j (c i) -> p c j i", i=4),
@@ -148,99 +174,97 @@ def tile_picked_softthr_none_p_kernel(
                 in_=w2_bf[h][:].rearrange("p m j -> p (m j)"),
             )
 
-        gaps = [[sb(f"gaps{t}_{h}", [P, 2, HALF], F32) for h in range(2)] for t in range(PACK)]
-
-        def look_up(t):
-            minus_d = [sb(f"minus_d{t}_{h}", [P, HALF], F32) for h in range(2)]
-            for h in range(2):
-                own = y_dup[0][h][:] if t == 0 else y_full[t - 1][:, half(h)]
-                nc.vector.tensor_tensor(minus_d[h][:], y_win[t][:].indirect(nb_sb[:, list_half(h)]), own, ALU.subtract)
-            if t == 0:
-                for h in range(2):
-                    nc.vector.tensor_tensor(gaps[t][h][:, 0, :], first_th[:, half(h)], minus_d[h][:], ALU.add)
-                    nc.vector.tensor_tensor(gaps[t][h][:, 1, :], first_th[:, half(h)], minus_d[h][:], ALU.subtract)
-                return minus_d
-            for h in range(2):
+        terms = sb("terms", [P, PACK, 2, HALF], F32)
+        turned_tags = [["bank5", "bank6"], ["bank7", "bank0"]]
+        turned = [
+            [psum.tile([P, PACK, P], F32, name=f"turned{k}_{s}", tag=turned_tags[k][s]) for s in range(2)]
+            for k in range(2)
+        ]
+        for t in range(PACK):
+            d = [sb(f"d{t}_{h}", [P, HALF], F32) for h in range(2)]
+            for h in (1, 0):
                 nc.vector.tensor_tensor(
-                    gaps[t][h][:, 0, :], tab_sb[t][:].indirect(kind_sb[:, list_half(h)]), minus_d[h][:], ALU.add
+                    d[h][:], y_win[t][:].indirect(nb_sb[:, list_half(h)]), y_own[t][:, half(h)], ALU.subtract
                 )
-            for h in range(2):
-                nc.vector.scalar_tensor_tensor(
-                    gaps[t][h][:, 1, :], minus_d[h][:], -2.0, gaps[t][h][:, 0, :], ALU.mult, ALU.add
-                )
-            return minus_d
-
-        def shrink(t):
-            for h in range(2):
-                nc.scalar.activation(shrunk[h][:, t], gaps[t][h][:], ACT.Relu, scale=minus_abs[:, t : t + 1])
-
-        leave_psum(1)
-        md0 = look_up(0)
-
-        leave_psum(2)
-        look_up(1)
-        shrink(0)
-        leave_psum(3)
-        look_up(2)
-        shrink(1)
-        weave_w2(0)
-        look_up(3)
-        shrink(2)
-        shrink(3)
-        weave_w2(1)
-
-        z_bf = [sb(f"z_bf{h}", [P, HALF, PACK], BF16) for h in range(2)]
-        z_codes = [sb(f"z_codes{h}", [P, HALF], U32) for h in range(2)]
-        z_scales = [sb(f"z_scales{h}", [P, HALF], U8) for h in range(2)]
-        o_tags = {0: ["bank5", "bank6"], 1: ["bank7", "bank0", "bank1", "bank2"]}
-        o_ps = {}
-
-        def make_z(h):
-            nc.vector.tensor_tensor(
-                z_bf[h][:].rearrange("p (c i) t -> p c t i", i=4),
-                shrunk[h][:, :, 0, :].rearrange("p t (c i) -> p c t i", i=4),
-                shrunk[h][:, :, 1, :].rearrange("p t (c i) -> p c t i", i=4),
-                ALU.subtract,
+            for k in range(2):
+                places = slice(k * P, (k + 1) * P)
+                for s in range(2):
+                    nc.tensor.matmul(
+                        turned[k][s][:, t, :], signed_th[t, s][:, places], identity[:],
+                        is_transpose=True, start=True, stop=False,
+                    )
+                    nc.tensor.matmul(
+                        turned[k][s][:, t, :], d[0][:, places], identity[:],
+                        is_transpose=True, start=False, stop=True,
+                    )
+            nc.vector.scalar_tensor_tensor(
+                terms[:, t, 0, :], th[t, 1], abs_gain[:, t : t + 1], d[1][:], ALU.mult, ALU.max
+            )
+            nc.vector.scalar_tensor_tensor(
+                terms[:, t, 1, :], th[t, 1], minus_abs[:, t : t + 1], d[1][:], ALU.mult, ALU.min
             )
 
-        def quantize_z(h):
-            nc.vector.quantize_mx(
-                out=z_codes[h][:].bitcast(FP8X4), scales=z_scales[h][:], in_=z_bf[h][:].rearrange("p j t -> p (j t)")
+        def turned_z(k):
+            above = sb(f"above{k}", [P, P, PACK], F32)
+            nc.scalar.activation(above[:], turned[k][0][:].rearrange("j t p -> j p t"), ACT.Relu)
+            z_turned = sb(f"z_turned{k}", [P, P, PACK], BF16)
+            nc.vector.scalar_tensor_tensor(
+                z_turned[:], turned[k][1][:].rearrange("j t p -> j p t"), 0.0, above[:], ALU.min, ALU.add
             )
+            words = z_turned[:].rearrange("j p t -> j (p t)").bitcast(F32)
+            back = psum.tile([P, 2, P], F32, name=f"back{k}", tag=f"bank{k + 1}")
+            for u in range(2):
+                nc.tensor.transpose(back[:, u, :], words[:, u : 2 * P : 2], identity[:])
+            z_bf = sb(f"z_bf{k}", [P, P * PACK], BF16)
+            nc.scalar.copy(
+                z_bf[:].bitcast(F32).rearrange("p (j u) -> p j u", u=2), back[:].rearrange("p u j -> p j u")
+            )
+            return z_bf
 
-        def second_product(h, b):
-            tiles = PACK // len(o_tags[h])
-            bank = psum.tile([P, tiles, HALF], F32, name=f"o_ps{h}_{b}", tag=o_tags[h][b])
+        def quantize_z(name, z_bf, width):
+            codes = sb(f"z_codes{name}", [P, width], U32)
+            scales = sb(f"z_scales{name}", [P, width], U8)
+            nc.vector.quantize_mx(out=codes[:].bitcast(FP8X4), scales=scales[:], in_=z_bf)
+            return codes, scales
+
+        def second_product(z, first_tile, tiles, width, tag):
+            bank = psum.tile([P, tiles, width], F32, name=f"o_{tag}", tag=tag)
             for c in range(tiles):
-                w_half, first = divmod((b * tiles + c) * P, HALF)
+                w_half, first = divmod((first_tile + c) * P, HALF)
                 cols = slice(first, first + P)
                 nc.tensor.matmul_mx(
                     out=bank[:, c, :], lhsT=w2_codes[w_half][:, cols].bitcast(FP8X4),
                     lhsT_scale=w2_scales[w_half][:, cols],
-                    rhs=z_codes[h][:].bitcast(FP8X4), rhs_scale=z_scales[h][:], start=True, stop=True,
+                    rhs=z[0][:].bitcast(FP8X4), rhs_scale=z[1][:], start=True, stop=True,
                 )
-            o_ps[h, b] = bank
+            return bank
 
-        def leave(h, b, queue):
-            tiles = PACK // len(o_tags[h])
-            pair, first = divmod(b * tiles, 2)
-            o_sb = sb(f"o_sb{h}_{b}", [P, tiles, HALF], F32)
-            nc.vector.tensor_tensor(
-                o_sb[:], o_ps[h, b][:], res_sb[pair][:, first : first + tiles, half(h)], ALU.add
-            )
-            queue.dma_start(out_rows[:, b * tiles : (b + 1) * tiles, half(h)], o_sb[:])
+        def leave(name, sums, pair, places, queue):
+            o_sb = sb(f"o_sb{name}", [P, 2, places.stop - places.start], F32)
+            nc.vector.tensor_tensor(o_sb[:], sums, res_sb[pair][:, :, places], ALU.add)
+            queue.dma_start(out_rows[:, 2 * pair : 2 * pair + 2, places], o_sb[:])
 
         quantize_w2(0)
-        make_z(0)
-        quantize_z(0)
-        second_product(0, 0)
-        make_z(1)
+        z_plain = sb("z_plain", [P, HALF, PACK], BF16)
+        nc.vector.tensor_tensor(
+            z_plain[:].rearrange("p (c i) t -> p c t i", i=4),
+            terms[:, :, 0, :].rearrange("p t (c i) -> p c t i", i=4),
+            terms[:, :, 1, :].rearrange("p t (c i) -> p c t i", i=4),
+            ALU.add,
+        )
         quantize_w2(1)
-        second_product(0, 1)
-        leave(0, 0, nc.sync)
-        quantize_z(1)
-        for b in range(PACK):
-            second_product(1, b)
-        leave(0, 1, nc.sync)
-        for b in range(PACK):
-            leave(1, b, nc.scalar if b % 2 else nc.sync)
+        z_block0 = turned_z(0)
+        z_second = quantize_z("second", z_plain[:].rearrange("p j t -> p (j t)"), HALF)
+        second_banks = [second_product(z_second, 2 * pair, 2, HALF, ("bank7", "bank6")[pair]) for pair in range(2)]
+        z_block1 = turned_z(1)
+        block_banks = []
+        for k, z_bf in enumerate((z_block0, z_block1)):
+            leave(f"second{k}", second_banks[k][:], k, half(1), nc.sync)
+            z = quantize_z(f"block{k}", z_bf[:], P)
+            block_banks.append([second_product(z, 2 * pair, 2, P, (("bank3", "bank4"), ("bank5", "bank0"))[k][pair]) for pair in range(2)])
+        for k in range(2):
+            for pair in range(2):
+                leave(
+                    f"block{k}_{pair}", block_banks[k][pair][:], pair, slice(k * P, (k + 1) * P),
+                    nc.scalar if pair else nc.sync,
+                )

from contextlib import ExitStack

import concourse.mybir as mybir
from concourse.masks import make_identity

K, T, S, N, H, U = 512, 2048, 512, 512, 512, 512
FLOPS = 2 * K * H * S + 2 * H * N * S

F32 = mybir.dt.float32
BF16 = mybir.dt.bfloat16
I32 = mybir.dt.int32
U32 = mybir.dt.uint32
U16 = mybir.dt.uint16
U8 = mybir.dt.uint8
FP8X4 = mybir.dt.float8_e4m3fn_x4
ALU = mybir.AluOpType
ACT = mybir.ActivationFunctionType

P = 128
PACK = 4
HALF = S // 2
LIST_HALF = HALF // 16
SCALAR_SHARE = 64
EARLY_TABLES = 3


def tile_picked_softthr_none_p_kernel(
    tc, x_words, x_scales, w1, tab, gn, w2, res, offs, kind, nb, out
):
    nc = tc.nc
    with ExitStack() as ctx:
        keep = ctx.enter_context(tc.tile_pool(name="keep", bufs=1))
        psum = ctx.enter_context(tc.psum_pool(name="psum", bufs=1))

        def sb(name, shape, dtype, tag=None):
            return keep.tile(shape, dtype, name=name, tag=tag or name, align_bytes=64)

        def half(h):
            return slice(h * HALF, (h + 1) * HALF)

        def list_half(h):
            return slice(h * LIST_HALF, (h + 1) * LIST_HALF)

        offs_sb = sb("offs_sb", [P, S // 16], U16)
        nb_sb = sb("nb_sb", [P, S // 16], U16)
        kind_sb = sb("kind_sb", [P, S // 16], U16)
        x_all = sb("x_all", [P, T], U32)
        xs_all = sb("xs_all", [P, T], U8)
        gain = sb("gain", [P, PACK], F32)
        w1_raw = sb("w1_raw", [P, PACK, H], F32)
        w2_raw = [sb(f"w2_raw{h}", [P, PACK, HALF], F32) for h in range(2)]
        tab_sb = [sb(f"tab{t}", [P, U], F32) for t in range(PACK)]
        res_sb = [sb(f"res{b}", [P, 2, S], F32) for b in range(2)]

        w2_rows = w2.rearrange("(p j) c -> p j c", j=PACK)
        tab_rows = tab.rearrange("(p t) c -> p t c", t=PACK)
        res_rows = res.rearrange("(c p) j -> p c j", p=P)
        out_rows = out.rearrange("(c p) j -> p c j", p=P)

        nc.vector.memset(xs_all[:, 0 : T // 2].bitcast(I32), 0)
        nc.gpsimd.memset(xs_all[:, T // 2 : T].bitcast(I32), 0)
        identity = sb("identity", [P, P], F32)
        make_identity(nc, identity[:])
        nc.scalar.dma_start(gain[:], gn.rearrange("(p t) o -> p (t o)", t=PACK))
        nc.sync.dma_start(kind_sb[:], kind)
        for t in range(EARLY_TABLES):
            nc.sync.dma_start(tab_sb[t][:], tab_rows[:, t, :])
        nc.sync.dma_start(w1_raw[:], w1.rearrange("(p j) c -> p j c", j=PACK))
        for q in range(4):
            nc.sync.dma_start(
                xs_all[32 * q : 32 * q + 4, :].bitcast(I32), x_scales[0, 4 * q : 4 * q + 4, :].bitcast(I32)
            )
        nc.sync.dma_start(offs_sb[:], offs)
        nc.sync.dma_start(x_all[:].bitcast(I32), x_words[0].rearrange("p n r -> p (n r)").bitcast(I32))
        for t in range(EARLY_TABLES, PACK):
            nc.sync.dma_start(tab_sb[t][:], tab_rows[:, t, :])
        nc.sync.dma_start(nb_sb[:], nb)
        for h in range(2):
            nc.sync.dma_start(w2_raw[h][:], w2_rows[:, :, half(h)])
        for b in range(2):
            nc.sync.dma_start(res_sb[b][:], res_rows[:, 2 * b : 2 * b + 2, :])

        early = [(0, 0), (1, 0), (2, 0), (0, 1), (1, 1)]
        late = [(3, 0), (2, 1), (3, 1)]
        th = {(t, h): sb(f"th{t}_{h}", [P, HALF], F32)[:] for t, h in early}

        def fetch_thresholds(t, h):
            nc.vector.tensor_copy(th[t, h], tab_sb[t][:].indirect(kind_sb[:, list_half(h)]))

        minus_gain = sb("minus_gain", [P, PACK], F32)
        abs_gain = sb("abs_gain", [P, PACK], F32)
        minus_abs = sb("minus_abs", [P, PACK], F32)
        nc.gpsimd.tensor_scalar(minus_gain[:], gain[:], -1.0, 0.0, ALU.mult, ALU.add)
        nc.scalar.activation(abs_gain[:], gain[:], ACT.Abs)
        nc.gpsimd.tensor_scalar(minus_abs[:], abs_gain[:], -1.0, 0.0, ALU.mult, ALU.add)
        signed_th = {(t, s): sb(f"signed_th{t}_{s}", [P, HALF], F32)[:] for t in (0,) for s in range(2)}

        def scale_thresholds(t):
            for s, factor in enumerate((minus_abs, abs_gain)):
                nc.scalar.activation(signed_th[t, s], th[t, 0], ACT.Copy, scale=factor[:, t : t + 1])

        for t, h in early:
            fetch_thresholds(t, h)
        scale_thresholds(0)

        w1_bf = sb("w1_bf", [P, PACK, P, PACK], BF16)
        w1_by_tile = w1_raw[:].rearrange("p j (m t) -> p m t j", t=PACK)
        w1_woven = w1_bf[:].rearrange("p t m j -> p m t j")
        nc.scalar.copy(w1_woven[:, 0:SCALAR_SHARE], w1_by_tile[:, 0:SCALAR_SHARE])
        nc.vector.tensor_copy(w1_woven[:, SCALAR_SHARE:P], w1_by_tile[:, SCALAR_SHARE:P])
        signed_mid = sb("signed_mid", [P, 2, 2, HALF], F32, tag="w1_raw")
        for t in (1, 2):
            for s in range(2):
                signed_th[t, s] = signed_mid[:, t - 1, s, :]
            scale_thresholds(t)
        xs_pick = sb("xs_pick", [P, S], U8)
        nc.vector.tensor_copy(xs_pick[:], xs_all[:].indirect(offs_sb[:]))
        w1_codes = sb("w1_codes", [P, H], U32, tag="xs_all")
        w1_scales = sb("w1_scales", [P, H], U8)
        nc.vector.quantize_mx(
            out=w1_codes[:].bitcast(FP8X4), scales=w1_scales[:], in_=w1_bf[:].rearrange("p t m j -> p (t m j)")
        )
        x_pick = sb("x_pick", [P, S], U32, tag="w1_bf")
        for h in (1, 0):
            nc.vector.tensor_copy(x_pick[:, half(h)], x_all[:].indirect(offs_sb[:, list_half(h)]))
        th_late = sb("th_late", [P, len(late), HALF], F32, tag="x_all")
        for place, key in enumerate(late):
            th[key] = th_late[:, place, :]

        def project(target, t, places):
            cols = slice(t * P, (t + 1) * P)
            nc.tensor.matmul_mx(
                out=target, lhsT=w1_codes[:, cols].bitcast(FP8X4), lhsT_scale=w1_scales[:, cols],
                rhs=x_pick[:, places].bitcast(FP8X4), rhs_scale=xs_pick[:, places], start=True, stop=True,
            )

        y_win = [sb(f"y_win{t}", [P, S], F32) for t in range(PACK)]
        y_own = [sb(f"y_own{t}", [P, S], F32) for t in range(PACK)]

        first_banks = [psum.tile([P, HALF], F32, name=f"y0_ps{h}", tag=f"bank{h}") for h in range(2)]
        for h in (1, 0):
            project(first_banks[h][:], 0, half(h))
        y_ps = [None]
        for t in range(1, PACK):
            bank = psum.tile([P, S], F32, name=f"y_ps{t}", tag=f"bank{t + 1}")
            project(bank[:], t, slice(0, S))
            y_ps.append(bank)
        for t, h in late:
            fetch_thresholds(t, h)
        for h in (1, 0):
            for copy in (y_win[0], y_own[0]):
                nc.scalar.activation(copy[:, half(h)], first_banks[h][:], ACT.Copy, scale=minus_gain[:, 0:1])
        for t in range(1, PACK):
            for copy in (y_win[t], y_own[t]):
                nc.scalar.activation(copy[:], y_ps[t][:], ACT.Copy, scale=minus_gain[:, t : t + 1])
            if t == 1:
                signed_late = sb("signed_late", [P, 2, HALF], F32, tag="xs_pick")
                for s in range(2):
                    signed_th[EARLY_TABLES, s] = signed_late[:, s, :]
                scale_thresholds(EARLY_TABLES)

        w2_bf = [sb(f"w2_bf{h}", [P, HALF, PACK], BF16, tag=("w1_bf", "xs_all")[h]) for h in range(2)]
        w2_codes = [sb(f"w2_codes{h}", [P, HALF], U32) for h in range(2)]
        w2_scales = [sb(f"w2_scales{h}", [P, HALF], U8) for h in range(2)]
        for h in range(2):
            nc.scalar.copy(
                w2_bf[h][:].rearrange("p (c i) j -> p c j i", i=4),
                w2_raw[h][:].rearrange("p j (c i) -> p c j i", i=4),
            )

        def quantize_w2(h):
            nc.vector.quantize_mx(
                out=w2_codes[h][:].bitcast(FP8X4), scales=w2_scales[h][:],
                in_=w2_bf[h][:].rearrange("p m j -> p (m j)"),
            )

        terms = sb("terms", [P, PACK, 2, HALF], F32)
        turned_tags = [["bank5", "bank6"], ["bank7", "bank0"]]
        turned = [
            [psum.tile([P, PACK, P], F32, name=f"turned{k}_{s}", tag=turned_tags[k][s]) for s in range(2)]
            for k in range(2)
        ]
        for t in range(PACK):
            d = [sb(f"d{t}_{h}", [P, HALF], F32) for h in range(2)]
            for h in (1, 0):
                nc.vector.tensor_tensor(
                    d[h][:], y_win[t][:].indirect(nb_sb[:, list_half(h)]), y_own[t][:, half(h)], ALU.subtract
                )
            for k in range(2):
                places = slice(k * P, (k + 1) * P)
                for s in range(2):
                    nc.tensor.matmul(
                        turned[k][s][:, t, :], signed_th[t, s][:, places], identity[:],
                        is_transpose=True, start=True, stop=False,
                    )
                    nc.tensor.matmul(
                        turned[k][s][:, t, :], d[0][:, places], identity[:],
                        is_transpose=True, start=False, stop=True,
                    )
            nc.vector.scalar_tensor_tensor(
                terms[:, t, 0, :], th[t, 1], abs_gain[:, t : t + 1], d[1][:], ALU.mult, ALU.max
            )
            nc.vector.scalar_tensor_tensor(
                terms[:, t, 1, :], th[t, 1], minus_abs[:, t : t + 1], d[1][:], ALU.mult, ALU.min
            )

        def turned_z(k):
            above = sb(f"above{k}", [P, P, PACK], F32)
            nc.scalar.activation(above[:], turned[k][0][:].rearrange("j t p -> j p t"), ACT.Relu)
            z_turned = sb(f"z_turned{k}", [P, P, PACK], BF16)
            nc.vector.scalar_tensor_tensor(
                z_turned[:], turned[k][1][:].rearrange("j t p -> j p t"), 0.0, above[:], ALU.min, ALU.add
            )
            words = z_turned[:].rearrange("j p t -> j (p t)").bitcast(F32)
            back = psum.tile([P, 2, P], F32, name=f"back{k}", tag=f"bank{k + 1}")
            for u in range(2):
                nc.tensor.transpose(back[:, u, :], words[:, u : 2 * P : 2], identity[:])
            z_bf = sb(f"z_bf{k}", [P, P * PACK], BF16)
            nc.scalar.copy(
                z_bf[:].bitcast(F32).rearrange("p (j u) -> p j u", u=2), back[:].rearrange("p u j -> p j u")
            )
            return z_bf

        def quantize_z(name, z_bf, width):
            codes = sb(f"z_codes{name}", [P, width], U32)
            scales = sb(f"z_scales{name}", [P, width], U8)
            nc.vector.quantize_mx(out=codes[:].bitcast(FP8X4), scales=scales[:], in_=z_bf)
            return codes, scales

        def second_product(z, first_tile, tiles, width, tag):
            bank = psum.tile([P, tiles, width], F32, name=f"o_{tag}", tag=tag)
            for c in range(tiles):
                w_half, first = divmod((first_tile + c) * P, HALF)
                cols = slice(first, first + P)
                nc.tensor.matmul_mx(
                    out=bank[:, c, :], lhsT=w2_codes[w_half][:, cols].bitcast(FP8X4),
                    lhsT_scale=w2_scales[w_half][:, cols],
                    rhs=z[0][:].bitcast(FP8X4), rhs_scale=z[1][:], start=True, stop=True,
                )
            return bank

        def leave(name, sums, pair, places, queue):
            o_sb = sb(f"o_sb{name}", [P, 2, places.stop - places.start], F32)
            nc.vector.tensor_tensor(o_sb[:], sums, res_sb[pair][:, :, places], ALU.add)
            queue.dma_start(out_rows[:, 2 * pair : 2 * pair + 2, places], o_sb[:])

        quantize_w2(0)
        z_plain = sb("z_plain", [P, HALF, PACK], BF16)
        nc.vector.tensor_tensor(
            z_plain[:].rearrange("p (c i) t -> p c t i", i=4),
            terms[:, :, 0, :].rearrange("p t (c i) -> p c t i", i=4),
            terms[:, :, 1, :].rearrange("p t (c i) -> p c t i", i=4),
            ALU.add,
        )
        quantize_w2(1)
        z_block0 = turned_z(0)
        z_second = quantize_z("second", z_plain[:].rearrange("p j t -> p (j t)"), HALF)
        second_banks = [second_product(z_second, 2 * pair, 2, HALF, ("bank7", "bank6")[pair]) for pair in range(2)]
        z_block1 = turned_z(1)
        block_banks = []
        for k, z_bf in enumerate((z_block0, z_block1)):
            leave(f"second{k}", second_banks[k][:], k, half(1), nc.sync)
            z = quantize_z(f"block{k}", z_bf[:], P)
            block_banks.append([second_product(z, 2 * pair, 2, P, (("bank3", "bank4"), ("bank5", "bank0"))[k][pair]) for pair in range(2)])
        for k in range(2):
            for pair in range(2):
                leave(
                    f"block{k}_{pair}", block_banks[k][pair][:], pair, slice(k * P, (k + 1) * P),
                    nc.scalar if pair else nc.sync,
                )
